import numpy as np
import ml_dtypes


def mxq(x, axis, fmt="e4m3"):
    dtype, down = {"e4m3": (ml_dtypes.float8_e4m3fn, 7), "e5m2": (ml_dtypes.float8_e5m2, 14)}[fmt]
    v = np.moveaxis(np.asarray(x, np.float32).astype(ml_dtypes.bfloat16).astype(np.float64), axis, -1)
    blocks = v.reshape(v.shape[:-1] + (-1, 32))
    amax = np.abs(blocks).max(-1, keepdims=True)
    byte = np.maximum(np.where(amax > 0, np.frexp(amax)[1] - 1 + 127, 0) - down, 1)
    scale = np.exp2(byte - 127.0)
    codes = (blocks / scale).astype(np.float32).astype(dtype).astype(np.float64)
    return np.moveaxis((codes * scale).reshape(v.shape), -1, axis)


WIDE = False


def mx_kscale(k):
    if not WIDE:
        return np.ones(k)
    levels = np.array([10, -10, 5, -5, 0])
    if k % 512:
        return np.exp2(np.random.permutation(np.resize(levels, k // 32))).repeat(32)
    a = np.empty((k // 512, 16))
    for p in range(k // 512):
        a[p, :8] = np.random.permutation(np.resize(levels, 8))
        for g in range(8):
            far = levels[np.abs(levels - a[p, g]) >= 10]
            a[p, g + 8] = far[np.random.randint(len(far))]
    return np.exp2(a.ravel()).repeat(32)


def f64(x):
    return np.asarray(x).astype(np.float64)


def striped(idx):
    return np.tile(idx.reshape(-1, 16).T, (8, 1)).astype(np.uint16)


def unstriped(offs):
    return offs[:16].T.reshape(-1).astype(np.int64)


def striped8(idx):
    return np.concatenate([x.reshape(-1, 16).T for x in idx]).astype(np.uint16)


def runs(offs, k):
    lists = np.stack([offs[16 * r : 16 * r + 16].T.reshape(-1) for r in range(8)]).astype(np.int64)
    return lists[np.arange(k) % 512 // 64]


def pack_weight(w):
    k, n = w.shape
    w = f64(np.asarray(w, np.float32).astype(ml_dtypes.bfloat16)).reshape(k // 32, 32, n)
    amax = np.abs(w).max(1)
    byte = np.clip(np.where(amax > 0, np.frexp(amax)[1] - 1 + 127 - 7, 1), 1, 254)
    scaled = (w * np.exp2(127.0 - byte)[:, None, :]).reshape(k, n).astype(np.float32)
    words = np.ascontiguousarray(scaled.reshape(k // 512, 128, 4, n).transpose(0, 1, 3, 2)).astype(ml_dtypes.float8_e4m3fn).view(np.uint8)
    return words, np.ascontiguousarray(byte.astype(np.uint8).reshape(k // 512, 16, n))


def unpack_weight(words, scales):
    g, p, n, _ = words.shape
    vals = np.ascontiguousarray(words).view(ml_dtypes.float8_e4m3fn).astype(np.float64) * np.repeat(np.exp2(scales.astype(np.float64) - 127.0), 8, axis=1)[..., None]
    return vals.transpose(0, 1, 3, 2).reshape(g * 512, n)

def planes(y):
    n, m = y.shape
    v = y.astype(np.float32).astype(ml_dtypes.bfloat16).astype(np.float64).reshape(n // 32, 32, m)
    top = np.abs(v).max(1)
    byte = np.clip(np.where(top > 0, np.frexp(top)[1] - 1 + 127 - 7, 1), 1, 254)
    codes = (v * np.exp2(127.0 - byte)[:, None, :]).reshape(n, m).astype(np.float32).astype(ml_dtypes.float8_e4m3fn).view(np.uint8)
    words = codes.reshape(n // 512, 128, 4, m).transpose(0, 1, 3, 2)
    return np.ascontiguousarray(words), np.ascontiguousarray(byte.astype(np.uint8).reshape(n // 512, 16, m))


K, T, S, G, H, C = 512, 1024, 512, 2048, 512, 512


def setup_inputs():
    n = np.random.standard_normal
    s = mx_kscale(K)[:, None]
    packed_xT = pack_weight(n((K, T)) * s)
    packed_dT = pack_weight(n((K, G)) / s)
    return {
        "x_words": packed_xT[0],
        "x_scales": packed_xT[1],
        "d_words": packed_dT[0],
        "d_scales": packed_dT[1],
        "gs": (np.random.uniform(0.5, 1.5, (K, 1)) / s).astype(np.float32),
        "offs": striped(np.random.permutation(T)[:S]),
        "k1": striped8(np.random.randint(0, G, (8, H))),
        "n1": striped8(np.stack([np.random.permutation(S) for _ in range(8)])),
        "n2": striped8(np.stack([np.random.permutation(S) for _ in range(8)])),
        "cand": striped(np.random.permutation(T)[:C]),
        "n3": striped8(np.stack([np.random.permutation(S) for _ in range(8)])),
        "n4": striped8(np.stack([np.random.permutation(S) for _ in range(8)])),
    }


def reference(x_words, x_scales, d_words, d_scales, gs, offs, k1, n1, n2, cand, n3, n4):
    x_cand = unpack_weight(x_words, x_scales)[:, unstriped(cand)]
    d_k1 = unpack_weight(d_words, d_scales)[np.arange(K)[:, None], runs(k1, K)]
    xq = unpack_weight(x_words, x_scales)[:, unstriped(offs)]
    h = 0.0625 * (d_k1.T @ xq)
    st = np.maximum(h, h[np.arange(H)[:, None], runs(n1, H)])
    z = f64(gs) * (np.minimum(st, st[np.arange(H)[:, None], runs(n2, H)]))
    s = 0.0625 * ((x_cand.T @ mxq(z, 0, "e4m3")))
    out_0 = np.minimum(np.maximum(s, s[np.arange(C)[:, None], runs(n3, C)]), s[np.arange(C)[:, None], runs(n4, C)])
    return (out_0,) + planes(out_0)

@@ -1,0 +1,200 @@
+from contextlib import ExitStack
+
+import concourse.mybir as mybir
+
+K, T, S, G, H, C = 512, 1024, 512, 2048, 512, 512
+FLOPS = 2 * K * H * S + 2 * K * C * S
+
+F32 = mybir.dt.float32
+BF16 = mybir.dt.bfloat16
+I32 = mybir.dt.int32
+U32 = mybir.dt.uint32
+U16 = mybir.dt.uint16
+U8 = mybir.dt.uint8
+FP8X4 = mybir.dt.float8_e4m3fn_x4
+COPY = mybir.ActivationFunctionType.Copy
+MAX = mybir.AluOpType.max
+MIN = mybir.AluOpType.min
+
+P = 128
+PACK = 4
+HALF = S // 2
+Z_PIECES = ((0, 256), (256, 384), (384, 512))
+OUT_PIECES = ((0, 256), (256, 384), (384, 512))
+
+
+def tile_picked_pqchopmnminmx_none_po_kernel(tc, x_words, x_scales, d_words, d_scales, gs, offs, k1, n1, n2, cand, n3, n4, out_0, out_1, out_2):
+    nc = tc.nc
+    with ExitStack() as ctx:
+        keep = ctx.enter_context(tc.tile_pool(name="keep", bufs=1))
+        psum = ctx.enter_context(tc.psum_pool(name="psum", bufs=1))
+
+        def load_list(src, name):
+            tile = keep.tile([P, S // 16], U16, name=name)
+            nc.sync.dma_start(tile[:], src)
+            return tile
+
+        def picked(window, offsets, a, b):
+            return window[:].indirect(offsets[:, a // 16 : b // 16])
+
+        def deal(src, dtype, name):
+            dealt = keep.tile([P, H], dtype, name=name, align_bytes=64)
+            nc.vector.tensor_copy(dealt[:].rearrange("p (t m) -> p t m", t=PACK), src[:].rearrange("p (m t) -> p t m", t=PACK))
+            return dealt
+
+        d_scale_win = keep.tile([P, G], U8, name="d_scale_win")
+        x_scale_win = keep.tile([P, T], U8, name="x_scale_win")
+        d_scale = keep.tile([P, H], U8, name="d_scale", align_bytes=64)
+        nc.gpsimd.memset(d_scale[:].bitcast(I32), 0)
+
+        k1_sb = load_list(k1, "k1_sb")
+        d_rows = d_scales[0].bitcast(I32)
+        nc.scalar.dma_start(d_scale_win[:].bitcast(I32), d_rows.unsqueeze(1).to_broadcast([16, 8, G // 4]))
+        offs_sb = load_list(offs, "offs_sb")
+        x_word_win = keep.tile([P, T], I32, name="x_word_win")
+        nc.sync.dma_start(x_word_win[:], x_words[0].rearrange("p n t -> p (n t)").bitcast(I32))
+        d_word_win = keep.tile([P, G], I32, name="d_word_win")
+        nc.sync.dma_start(d_word_win[:], d_words[0].rearrange("p n t -> p (n t)").bitcast(I32))
+        x_rows = x_scales[0].bitcast(I32)
+        for r in range(4):
+            nc.scalar.dma_start(x_scale_win[:].bitcast(I32)[r:P:4, :], x_rows[r:16:4, :].unsqueeze(1).to_broadcast([4, 8, T // 4]))
+
+        warm = keep.tile([P, 2], F32, name="warm")
+        nc.gpsimd.memset(warm[:, 0:1], 0.0)
+        nc.scalar.activation(warm[:, 1:2], warm[:, 0:1], COPY, scale=0.0625)
+
+        def gather_packed(window, offsets, dtype, name):
+            got = keep.tile([P, S], dtype, name=name, align_bytes=64)
+            nc.vector.tensor_copy(got[:], window[:].bitcast(dtype).indirect(offsets[:]))
+            return got
+
+        d_scale_got = gather_packed(d_scale_win, k1_sb, U8, "d_scale_got")
+        xq_words = gather_packed(x_word_win, offs_sb, U32, "xq_words")
+        d_scale_dealt = deal(d_scale_got, U8, "d_scale_dealt")
+        for j in range(4):
+            queue = nc.sync if j % 2 == 0 else nc.scalar
+            first = 8 * j
+            queue.dma_start(d_scale[:].bitcast(I32)[j:P:32, :], d_scale_dealt[:].bitcast(I32)[first:P:32, :])
+        cand_sb = load_list(cand, "cand_sb")
+        n1_sb = load_list(n1, "n1_sb")
+        n2_sb = load_list(n2, "n2_sb")
+        gs_sb = keep.tile([P, PACK], F32, name="gs_sb")
+        nc.gpsimd.dma_start(gs_sb[:], gs.rearrange("(p t) o -> p (t o)", t=PACK))
+        n3_sb = load_list(n3, "n3_sb")
+        n4_sb = load_list(n4, "n4_sb")
+
+        d_words_got = gather_packed(d_word_win, k1_sb, U32, "d_words_got")
+        xq_scale = gather_packed(x_scale_win, offs_sb, U8, "xq_scale")
+        d_codes = deal(d_words_got, U32, "d_codes")
+
+        h = []
+        for t in range(PACK):
+            rows = slice(P * t, P * (t + 1))
+            acc = psum.tile([P, S], F32, name="acc_h%d" % t, tag="bank%d" % t)
+            nc.tensor.matmul_mx(out=acc[:], lhsT=d_codes[:, rows].bitcast(FP8X4), lhsT_scale=d_scale[:, rows], rhs=xq_words[:].bitcast(FP8X4), rhs_scale=xq_scale[:], start=True, stop=True)
+            h_t = keep.tile([P, 2 * S], F32, name="h%d" % t)
+            nc.scalar.activation(h_t[:, 0:S], acc[:], COPY, scale=0.0625)
+            h.append(h_t)
+
+        c_scale_got = gather_packed(x_scale_win, cand_sb, U8, "c_scale_got")
+        c_words_got = gather_packed(x_word_win, cand_sb, U32, "c_words_got")
+        c_scale = deal(c_scale_got, U8, "c_scale")
+        c_codes = deal(c_words_got, U32, "c_codes")
+
+        h_at_n1 = [keep.tile([P, S], F32, name="h_at_n1_%d" % t) for t in range(PACK)]
+        st = [keep.tile([P, S], F32, name="st%d" % t) for t in range(PACK)]
+
+        def fetch_n1(t):
+            nc.vector.tensor_copy(h_at_n1[t][:], picked(h[t], n1_sb, 0, S))
+
+        def larger(t):
+            nc.vector.tensor_tensor(st[t][:], h[t][:, 0:S], h_at_n1[t][:], MAX)
+
+        fetch_n1(0)
+        for t in range(1, PACK):
+            fetch_n1(t)
+            larger(t - 1)
+
+        s = [keep.tile([P, S], F32, name="s%d" % t) for t in range(PACK)]
+        z_grouped = [keep.tile([P, b - a, PACK], BF16, name="z_grouped%d" % a, align_bytes=64) for a, b in Z_PIECES]
+        st_at_n2 = {}
+
+        def fetch_n2(i, t):
+            a, b = Z_PIECES[i]
+            st_at_n2[i, t] = keep.tile([P, b - a], F32, name="st_at_n2_%d_%d" % (i, t))
+            nc.vector.tensor_copy(st_at_n2[i, t][:], picked(st[t], n2_sb, a, b))
+
+        def smaller_weighted(i, t):
+            a, b = Z_PIECES[i]
+            least = keep.tile([P, b - a], F32, name="least_%d_%d" % (i, t))
+            nc.vector.tensor_tensor(least[:], st[t][:, a:b], st_at_n2[i, t][:], MIN)
+            nc.scalar.activation(z_grouped[i][:, :, t], least[:], COPY, scale=gs_sb[:, t : t + 1])
+
+        def score(i):
+            a, b = Z_PIECES[i]
+            z_codes = keep.tile([P, b - a], U32, name="z_codes%d" % i, align_bytes=64)
+            z_scale = keep.tile([P, b - a], U8, name="z_scale%d" % i, align_bytes=64)
+            nc.vector.quantize_mx(out=z_codes[:].bitcast(FP8X4), scales=z_scale[:], in_=z_grouped[i][:].rearrange("p c t -> p (c t)"))
+            for pair in range(2):
+                acc = psum.tile([P, 2, b - a], F32, name="acc_s%d_%d" % (i, pair), tag="bank%d" % ((4 + 2 * i + pair) % 8))
+                for u in range(2):
+                    t = 2 * pair + u
+                    rows = slice(P * t, P * (t + 1))
+                    nc.tensor.matmul_mx(out=acc[:, u, :], lhsT=c_codes[:, rows].bitcast(FP8X4), lhsT_scale=c_scale[:, rows], rhs=z_codes[:].bitcast(FP8X4), rhs_scale=z_scale[:], start=True, stop=True)
+                for u in range(2):
+                    nc.scalar.activation(s[2 * pair + u][:, a:b], acc[:, u, :], COPY, scale=0.0625)
+
+        steps = [(i, t) for i in range(len(Z_PIECES)) for t in range(PACK)]
+        fetch_n2(*steps[0])
+        larger(PACK - 1)
+        for n in range(1, len(steps)):
+            fetch_n2(*steps[n])
+            smaller_weighted(*steps[n - 1])
+            if steps[n][0] > 0 and steps[n][1] == 2:
+                score(steps[n][0] - 1)
+        smaller_weighted(*steps[-1])
+        score(len(Z_PIECES) - 1)
+
+        out_rows = out_0.rearrange("(p t) c -> p t c", t=PACK)
+        out_words = out_1[0].rearrange("p n t -> p (n t)").bitcast(I32)
+        out_scale = keep.tile([P, S], U8, name="out_scale", align_bytes=64)
+        result = [keep.tile([P, PACK, b - a], F32, name="result%d" % a) for a, b in OUT_PIECES]
+        out_grouped = [keep.tile([P, b - a, PACK], BF16, name="out_grouped%d" % a, align_bytes=64) for a, b in OUT_PIECES]
+        s_at_n3, s_at_n4, upper = {}, {}, {}
+
+        def fetch(store, offsets, name, i, t):
+            a, b = OUT_PIECES[i]
+            store[i, t] = keep.tile([P, b - a], F32, name="%s_%d_%d" % (name, i, t))
+            nc.vector.tensor_copy(store[i, t][:], picked(s[t], offsets, a, b))
+
+        def raise_to_n3(i, t):
+            a, b = OUT_PIECES[i]
+            upper[i, t] = keep.tile([P, b - a], F32, name="upper_%d_%d" % (i, t))
+            nc.vector.tensor_tensor(upper[i, t][:], s[t][:, a:b], s_at_n3[i, t][:], MAX)
+
+        def cap_at_n4(i, t):
+            nc.vector.tensor_tensor(result[i][:, t, :], upper[i, t][:], s_at_n4[i, t][:], MIN)
+            nc.scalar.copy(out_grouped[i][:, :, t], result[i][:, t, :])
+
+        def hand_out(i):
+            a, b = OUT_PIECES[i]
+            nc.sync.dma_start(out_rows[:, :, a:b], result[i][:])
+            codes = keep.tile([P, b - a], I32, name="out_codes%d" % i, align_bytes=64)
+            nc.vector.quantize_mx(out=codes[:].bitcast(FP8X4), scales=out_scale[:, a:b], in_=out_grouped[i][:].rearrange("p c t -> p (c t)"))
+            nc.sync.dma_start(out_words[:, a:b], codes[:])
+
+        steps = [(i, t) for i in range(len(OUT_PIECES)) for t in range(PACK)]
+        for n in range(len(steps)):
+            fetch(s_at_n3, n3_sb, "s_at_n3", *steps[n])
+            if n > 0:
+                cap_at_n4(*steps[n - 1])
+            fetch(s_at_n4, n4_sb, "s_at_n4", *steps[n])
+            raise_to_n3(*steps[n])
+            if steps[n][0] > 0 and steps[n][1] == 1:
+                hand_out(steps[n][0] - 1)
+        cap_at_n4(*steps[-1])
+        hand_out(len(OUT_PIECES) - 1)
+        scale_rows = out_2[0].bitcast(I32)
+        for q in range(4):
+            queue = nc.scalar if q % 2 == 0 else nc.sync
+            queue.dma_start(scale_rows[4 * q : 4 * q + 4, :], out_scale[:].bitcast(I32)[32 * q : 32 * q + 4, :])

@@ -18,9 +18,8 @@ MIN = mybir.AluOpType.min
 
 P = 128
 PACK = 4
-HALF = S // 2
-Z_PIECES = ((0, 256), (256, 384), (384, 512))
-OUT_PIECES = ((0, 256), (256, 384), (384, 512))
+LAST = PACK - 1
+PIECES = ((0, 256), (256, 384), (384, 512))
 
 
 def tile_picked_pqchopmnminmx_none_po_kernel(tc, x_words, x_scales, d_words, d_scales, gs, offs, k1, n1, n2, cand, n3, n4, out_0, out_1, out_2):
@@ -37,163 +36,159 @@ def tile_picked_pqchopmnminmx_none_po_kernel(tc, x_words, x_scales, d_words, d_s
         def picked(window, offsets, a, b):
             return window[:].indirect(offsets[:, a // 16 : b // 16])
 
+        def window(name, t):
+            return keep.tile([P, S if t == LAST else 2 * S], F32, name="%s%d" % (name, t))
+
         def deal(src, dtype, name):
             dealt = keep.tile([P, H], dtype, name=name, align_bytes=64)
-            nc.vector.tensor_copy(dealt[:].rearrange("p (t m) -> p t m", t=PACK), src[:].rearrange("p (m t) -> p t m", t=PACK))
+            nc.vector.tensor_copy(dealt[:].rearrange("p (t m) -> p m t", t=PACK), src[:].rearrange("p (m t) -> p m t", t=PACK))
             return dealt
 
-        d_scale_win = keep.tile([P, G], U8, name="d_scale_win")
-        x_scale_win = keep.tile([P, T], U8, name="x_scale_win")
         d_scale = keep.tile([P, H], U8, name="d_scale", align_bytes=64)
         nc.gpsimd.memset(d_scale[:].bitcast(I32), 0)
 
         k1_sb = load_list(k1, "k1_sb")
-        d_rows = d_scales[0].bitcast(I32)
-        nc.scalar.dma_start(d_scale_win[:].bitcast(I32), d_rows.unsqueeze(1).to_broadcast([16, 8, G // 4]))
+        d_scale_win = keep.tile([P, G], U8, name="d_scale_win")
+        nc.sync.dma_start(d_scale_win[:].bitcast(I32), d_scales[0].bitcast(I32).unsqueeze(1).to_broadcast([16, 8, G // 4]))
         offs_sb = load_list(offs, "offs_sb")
         x_word_win = keep.tile([P, T], I32, name="x_word_win")
         nc.sync.dma_start(x_word_win[:], x_words[0].rearrange("p n t -> p (n t)").bitcast(I32))
+        x_scale_win = keep.tile([P, T], U8, name="x_scale_win")
+        x_rows = x_scales[0].bitcast(I32)
+        for q in range(4):
+            nc.sync.dma_start(x_scale_win[:].bitcast(I32)[32 * q : 32 * q + 32, :], x_rows[4 * q : 4 * q + 4, :].unsqueeze(0).to_broadcast([8, 4, T // 4]))
         d_word_win = keep.tile([P, G], I32, name="d_word_win")
         nc.sync.dma_start(d_word_win[:], d_words[0].rearrange("p n t -> p (n t)").bitcast(I32))
-        x_rows = x_scales[0].bitcast(I32)
-        for r in range(4):
-            nc.scalar.dma_start(x_scale_win[:].bitcast(I32)[r:P:4, :], x_rows[r:16:4, :].unsqueeze(1).to_broadcast([4, 8, T // 4]))
 
-        warm = keep.tile([P, 2], F32, name="warm")
-        nc.gpsimd.memset(warm[:, 0:1], 0.0)
-        nc.scalar.activation(warm[:, 1:2], warm[:, 0:1], COPY, scale=0.0625)
+        gs_sb = keep.tile([P, PACK], F32, name="gs_sb")
+        nc.gpsimd.dma_start(gs_sb[:], gs.rearrange("(p t) o -> p (t o)", t=PACK))
+        gs_size = keep.tile([P, PACK], F32, name="gs_size")
+        gs_sign = keep.tile([P, PACK], F32, name="gs_sign")
+        nc.scalar.activation(gs_size[:], gs_sb[:], mybir.ActivationFunctionType.Abs, scale=0.0625)
+        nc.scalar.activation(gs_sign[:], gs_sb[:], mybir.ActivationFunctionType.Sign)
 
-        def gather_packed(window, offsets, dtype, name):
-            got = keep.tile([P, S], dtype, name=name, align_bytes=64)
-            nc.vector.tensor_copy(got[:], window[:].bitcast(dtype).indirect(offsets[:]))
+        def gather_packed(table, offsets, dtype, name, tag):
+            got = keep.tile([P, S], dtype, name=name, tag=tag, align_bytes=64)
+            nc.vector.tensor_copy(got[:], table[:].bitcast(dtype).indirect(offsets[:]))
             return got
 
-        d_scale_got = gather_packed(d_scale_win, k1_sb, U8, "d_scale_got")
-        xq_words = gather_packed(x_word_win, offs_sb, U32, "xq_words")
+        d_scale_got = gather_packed(d_scale_win, k1_sb, U8, "d_scale_got", "d_scale_got")
         d_scale_dealt = deal(d_scale_got, U8, "d_scale_dealt")
         for j in range(4):
-            queue = nc.sync if j % 2 == 0 else nc.scalar
-            first = 8 * j
-            queue.dma_start(d_scale[:].bitcast(I32)[j:P:32, :], d_scale_dealt[:].bitcast(I32)[first:P:32, :])
+            nc.scalar.dma_start(d_scale[:].bitcast(I32)[j:P:32, :], d_scale_dealt[:].bitcast(I32)[8 * j : P : 32, :])
         cand_sb = load_list(cand, "cand_sb")
         n1_sb = load_list(n1, "n1_sb")
         n2_sb = load_list(n2, "n2_sb")
-        gs_sb = keep.tile([P, PACK], F32, name="gs_sb")
-        nc.gpsimd.dma_start(gs_sb[:], gs.rearrange("(p t) o -> p (t o)", t=PACK))
         n3_sb = load_list(n3, "n3_sb")
         n4_sb = load_list(n4, "n4_sb")
 
-        d_words_got = gather_packed(d_word_win, k1_sb, U32, "d_words_got")
-        xq_scale = gather_packed(x_scale_win, offs_sb, U8, "xq_scale")
+        xq_words = gather_packed(x_word_win, offs_sb, U32, "xq_words", "xq_words")
+        xq_scale = gather_packed(x_scale_win, offs_sb, U8, "xq_scale", "xq_scale")
+        d_words_got = gather_packed(d_word_win, k1_sb, U32, "d_words_got", "after_d")
         d_codes = deal(d_words_got, U32, "d_codes")
 
-        h = []
-        for t in range(PACK):
+        def product(lhs_codes, lhs_scale, t, rhs_codes, rhs_scale, a, b, bank, dest, scale):
             rows = slice(P * t, P * (t + 1))
-            acc = psum.tile([P, S], F32, name="acc_h%d" % t, tag="bank%d" % t)
-            nc.tensor.matmul_mx(out=acc[:], lhsT=d_codes[:, rows].bitcast(FP8X4), lhsT_scale=d_scale[:, rows], rhs=xq_words[:].bitcast(FP8X4), rhs_scale=xq_scale[:], start=True, stop=True)
-            h_t = keep.tile([P, 2 * S], F32, name="h%d" % t)
-            nc.scalar.activation(h_t[:, 0:S], acc[:], COPY, scale=0.0625)
-            h.append(h_t)
+            acc = psum.tile([P, b - a], F32, name="acc", tag="bank%d" % bank)
+            nc.tensor.matmul_mx(out=acc[:], lhsT=lhs_codes[:, rows].bitcast(FP8X4), lhsT_scale=lhs_scale[:, rows], rhs=rhs_codes[:, a:b].bitcast(FP8X4), rhs_scale=rhs_scale[:, a:b], start=True, stop=True)
+            nc.scalar.activation(dest[:, a:b], acc[:], COPY, scale=scale)
 
-        c_scale_got = gather_packed(x_scale_win, cand_sb, U8, "c_scale_got")
-        c_words_got = gather_packed(x_word_win, cand_sb, U32, "c_words_got")
+        h = [keep.tile([P, 2 * S], F32, name="h%d" % t) for t in range(PACK)]
+        for t in range(PACK):
+            product(d_codes, d_scale, t, xq_words, xq_scale, 0, S, t, h[t], gs_size[:, t : t + 1])
+
+        c_scale_got = gather_packed(x_scale_win, cand_sb, U8, "c_scale_got", "after_d")
         c_scale = deal(c_scale_got, U8, "c_scale")
-        c_codes = deal(c_words_got, U32, "c_codes")
 
-        h_at_n1 = [keep.tile([P, S], F32, name="h_at_n1_%d" % t) for t in range(PACK)]
-        st = [keep.tile([P, S], F32, name="st%d" % t) for t in range(PACK)]
+        st = [window("st", t) for t in range(PACK)]
+        z_grouped = [keep.tile([P, b - a, PACK], BF16, name="z_grouped%d" % a, align_bytes=64) for a, b in PIECES]
+        st_rounded = [keep.tile([P, S], BF16, name="st_rounded%d" % t) for t in range(PACK)]
+        fetched = {}
 
-        def fetch_n1(t):
-            nc.vector.tensor_copy(h_at_n1[t][:], picked(h[t], n1_sb, 0, S))
+        def fetch(src, offsets, name, t, a, b, tag=None):
+            dtype = BF16 if name == "n2" else F32
+            key = "%s_%d_%d" % (name, t, a)
+            fetched[name, t, a] = keep.tile([P, b - a], dtype, name=key, tag=tag or key, align_bytes=64)
+            nc.vector.tensor_copy(fetched[name, t, a][:], picked(src[t], offsets, a, b))
+
+        def regroup(grouped, values, t, a, b, scale):
+            for i, (pa, pb) in enumerate(PIECES):
+                if a <= pa and pb <= b:
+                    nc.scalar.activation(grouped[i][:, :, t], values[:, pa - a : pb - a], COPY, scale=scale)
 
         def larger(t):
-            nc.vector.tensor_tensor(st[t][:], h[t][:, 0:S], h_at_n1[t][:], MAX)
+            nc.vector.tensor_tensor(st[t][:, 0:S], h[t][:, 0:S], fetched["n1", t, 0][:], MAX)
+            nc.scalar.copy(st_rounded[t][:], st[t][:, 0:S])
 
-        fetch_n1(0)
+        def smaller_weighted(t, a, b):
+            least = keep.tile([P, b - a], BF16, name="least_%d_%d" % (t, a))
+            nc.vector.tensor_tensor(least[:], st_rounded[t][:, a:b], fetched["n2", t, a][:], MIN)
+            regroup(z_grouped, least, t, a, b, gs_sign[:, t : t + 1])
+
+        fetch(h, n1_sb, "n1", 0, 0, S)
+        larger(0)
         for t in range(1, PACK):
-            fetch_n1(t)
-            larger(t - 1)
+            fetch(h, n1_sb, "n1", t, 0, S)
+            fetch(st, n2_sb, "n2", t - 1, 0, S)
+            larger(t)
+            smaller_weighted(t - 1, 0, S)
+        first, second, third = PIECES
+        fetch(st, n2_sb, "n2", LAST, *first)
+        fetch(st, n2_sb, "n2", LAST, *second, tag="after_z")
+        smaller_weighted(LAST, *first)
+        fetch(st, n2_sb, "n2", LAST, *third)
+        smaller_weighted(LAST, *second)
+        smaller_weighted(LAST, *third)
 
-        s = [keep.tile([P, S], F32, name="s%d" % t) for t in range(PACK)]
-        z_grouped = [keep.tile([P, b - a, PACK], BF16, name="z_grouped%d" % a, align_bytes=64) for a, b in Z_PIECES]
-        st_at_n2 = {}
+        z_codes = keep.tile([P, S], U32, name="z_codes", align_bytes=64)
+        z_scale = keep.tile([P, S], U8, name="z_scale", align_bytes=64)
 
-        def fetch_n2(i, t):
-            a, b = Z_PIECES[i]
-            st_at_n2[i, t] = keep.tile([P, b - a], F32, name="st_at_n2_%d_%d" % (i, t))
-            nc.vector.tensor_copy(st_at_n2[i, t][:], picked(st[t], n2_sb, a, b))
+        def quantize(codes, scales, grouped):
+            nc.vector.quantize_mx(out=codes.bitcast(FP8X4), scales=scales, in_=grouped[:].rearrange("p c t -> p (c t)"))
 
-        def smaller_weighted(i, t):
-            a, b = Z_PIECES[i]
-            least = keep.tile([P, b - a], F32, name="least_%d_%d" % (i, t))
-            nc.vector.tensor_tensor(least[:], st[t][:, a:b], st_at_n2[i, t][:], MIN)
-            nc.scalar.activation(z_grouped[i][:, :, t], least[:], COPY, scale=gs_sb[:, t : t + 1])
-
-        def score(i):
-            a, b = Z_PIECES[i]
-            z_codes = keep.tile([P, b - a], U32, name="z_codes%d" % i, align_bytes=64)
-            z_scale = keep.tile([P, b - a], U8, name="z_scale%d" % i, align_bytes=64)
-            nc.vector.quantize_mx(out=z_codes[:].bitcast(FP8X4), scales=z_scale[:], in_=z_grouped[i][:].rearrange("p c t -> p (c t)"))
-            for pair in range(2):
-                acc = psum.tile([P, 2, b - a], F32, name="acc_s%d_%d" % (i, pair), tag="bank%d" % ((4 + 2 * i + pair) % 8))
-                for u in range(2):
-                    t = 2 * pair + u
-                    rows = slice(P * t, P * (t + 1))
-                    nc.tensor.matmul_mx(out=acc[:, u, :], lhsT=c_codes[:, rows].bitcast(FP8X4), lhsT_scale=c_scale[:, rows], rhs=z_codes[:].bitcast(FP8X4), rhs_scale=z_scale[:], start=True, stop=True)
-                for u in range(2):
-                    nc.scalar.activation(s[2 * pair + u][:, a:b], acc[:, u, :], COPY, scale=0.0625)
-
-        steps = [(i, t) for i in range(len(Z_PIECES)) for t in range(PACK)]
-        fetch_n2(*steps[0])
-        larger(PACK - 1)
-        for n in range(1, len(steps)):
-            fetch_n2(*steps[n])
-            smaller_weighted(*steps[n - 1])
-            if steps[n][0] > 0 and steps[n][1] == 2:
-                score(steps[n][0] - 1)
-        smaller_weighted(*steps[-1])
-        score(len(Z_PIECES) - 1)
+        c_words_got = gather_packed(x_word_win, cand_sb, U32, "c_words_got", "after_z")
+        s = [window("s", t) for t in range(PACK)]
+        for i, (a, b) in enumerate(PIECES):
+            quantize(z_codes[:, a:b], z_scale[:, a:b], z_grouped[i])
+            if i == 0:
+                c_codes = deal(c_words_got, U32, "c_codes")
+            product(c_codes, c_scale, 0, z_codes, z_scale, a, b, 4 + i, s[0], 0.0625)
+        for t in range(1, PACK):
+            product(c_codes, c_scale, t, z_codes, z_scale, 0, S, (6 + t) % 8, s[t], 0.0625)
 
         out_rows = out_0.rearrange("(p t) c -> p t c", t=PACK)
         out_words = out_1[0].rearrange("p n t -> p (n t)").bitcast(I32)
         out_scale = keep.tile([P, S], U8, name="out_scale", align_bytes=64)
-        result = [keep.tile([P, PACK, b - a], F32, name="result%d" % a) for a, b in OUT_PIECES]
-        out_grouped = [keep.tile([P, b - a, PACK], BF16, name="out_grouped%d" % a, align_bytes=64) for a, b in OUT_PIECES]
-        s_at_n3, s_at_n4, upper = {}, {}, {}
+        out_grouped = [keep.tile([P, b - a, PACK], BF16, name="out_grouped%d" % a, align_bytes=64) for a, b in PIECES]
+        upper = {}
 
-        def fetch(store, offsets, name, i, t):
-            a, b = OUT_PIECES[i]
-            store[i, t] = keep.tile([P, b - a], F32, name="%s_%d_%d" % (name, i, t))
-            nc.vector.tensor_copy(store[i, t][:], picked(s[t], offsets, a, b))
+        def raise_to_n3(t, a, b):
+            upper[t, a] = keep.tile([P, b - a], F32, name="upper_%d_%d" % (t, a))
+            nc.vector.tensor_tensor(upper[t, a][:], s[t][:, a:b], fetched["n3", t, a][:], MAX)
 
-        def raise_to_n3(i, t):
-            a, b = OUT_PIECES[i]
-            upper[i, t] = keep.tile([P, b - a], F32, name="upper_%d_%d" % (i, t))
-            nc.vector.tensor_tensor(upper[i, t][:], s[t][:, a:b], s_at_n3[i, t][:], MAX)
-
-        def cap_at_n4(i, t):
-            nc.vector.tensor_tensor(result[i][:, t, :], upper[i, t][:], s_at_n4[i, t][:], MIN)
-            nc.scalar.copy(out_grouped[i][:, :, t], result[i][:, t, :])
+        def cap_at_n4(t, a, b):
+            result = keep.tile([P, b - a], F32, name="result_%d_%d" % (t, a))
+            nc.vector.tensor_tensor(result[:], upper[t, a][:], fetched["n4", t, a][:], MIN)
+            regroup(out_grouped, result, t, a, b, 1.0)
+            nc.sync.dma_start(out_rows[:, t, a:b], result[:])
 
         def hand_out(i):
-            a, b = OUT_PIECES[i]
-            nc.sync.dma_start(out_rows[:, :, a:b], result[i][:])
+            a, b = PIECES[i]
             codes = keep.tile([P, b - a], I32, name="out_codes%d" % i, align_bytes=64)
-            nc.vector.quantize_mx(out=codes[:].bitcast(FP8X4), scales=out_scale[:, a:b], in_=out_grouped[i][:].rearrange("p c t -> p (c t)"))
+            quantize(codes[:], out_scale[:, a:b], out_grouped[i])
             nc.sync.dma_start(out_words[:, a:b], codes[:])
 
-        steps = [(i, t) for i in range(len(OUT_PIECES)) for t in range(PACK)]
-        for n in range(len(steps)):
-            fetch(s_at_n3, n3_sb, "s_at_n3", *steps[n])
+        steps = [(t, 0, S) for t in range(LAST)] + [(LAST, a, b) for a, b in PIECES]
+        for n, step in enumerate(steps):
+            fetch(s, n3_sb, "n3", *step)
             if n > 0:
                 cap_at_n4(*steps[n - 1])
-            fetch(s_at_n4, n4_sb, "s_at_n4", *steps[n])
-            raise_to_n3(*steps[n])
-            if steps[n][0] > 0 and steps[n][1] == 1:
-                hand_out(steps[n][0] - 1)
+            fetch(s, n4_sb, "n4", *step)
+            raise_to_n3(*step)
+        hand_out(0)
         cap_at_n4(*steps[-1])
-        hand_out(len(OUT_PIECES) - 1)
+        hand_out(1)
+        hand_out(2)
         scale_rows = out_2[0].bitcast(I32)
         for q in range(4):
             queue = nc.scalar if q % 2 == 0 else nc.sync

@@ -39,10 +39,10 @@ def tile_picked_pqchopmnminmx_none_po_kernel(tc, x_words, x_scales, d_words, d_s
         def window(name, t):
             return keep.tile([P, S if t == LAST else 2 * S], F32, name="%s%d" % (name, t))
 
-        def deal(src, dtype, name):
-            dealt = keep.tile([P, H], dtype, name=name, align_bytes=64)
-            nc.vector.tensor_copy(dealt[:].rearrange("p (t m) -> p m t", t=PACK), src[:].rearrange("p (m t) -> p m t", t=PACK))
-            return dealt
+        def deal(src, dtype, name, t0=0, t1=PACK, tag=None):
+            dealt = keep.tile([P, t1 - t0, P], dtype, name=name, tag=tag or name, align_bytes=64)
+            nc.vector.tensor_copy(dealt[:].rearrange("p t m -> p m t"), src[:].rearrange("p (m t) -> p m t", t=PACK)[:, :, t0:t1])
+            return [dealt[:, t, :] for t in range(t1 - t0)]
 
         d_scale = keep.tile([P, H], U8, name="d_scale", align_bytes=64)
         nc.gpsimd.memset(d_scale[:].bitcast(I32), 0)
@@ -73,7 +73,8 @@ def tile_picked_pqchopmnminmx_none_po_kernel(tc, x_words, x_scales, d_words, d_s
             return got
 
         d_scale_got = gather_packed(d_scale_win, k1_sb, U8, "d_scale_got", "d_scale_got")
-        d_scale_dealt = deal(d_scale_got, U8, "d_scale_dealt")
+        d_scale_dealt = keep.tile([P, H], U8, name="d_scale_dealt")
+        nc.vector.tensor_copy(d_scale_dealt[:].rearrange("p (t m) -> p m t", t=PACK), d_scale_got[:].rearrange("p (m t) -> p m t", t=PACK))
         for j in range(4):
             nc.scalar.dma_start(d_scale[:].bitcast(I32)[j:P:32, :], d_scale_dealt[:].bitcast(I32)[8 * j : P : 32, :])
         cand_sb = load_list(cand, "cand_sb")
@@ -85,23 +86,22 @@ def tile_picked_pqchopmnminmx_none_po_kernel(tc, x_words, x_scales, d_words, d_s
         xq_words = gather_packed(x_word_win, offs_sb, U32, "xq_words", "xq_words")
         xq_scale = gather_packed(x_scale_win, offs_sb, U8, "xq_scale", "xq_scale")
         d_words_got = gather_packed(d_word_win, k1_sb, U32, "d_words_got", "after_d")
-        d_codes = deal(d_words_got, U32, "d_codes")
+        d_codes = deal(d_words_got, U32, "d_codes_first", 0, 1) + deal(d_words_got, U32, "d_codes_rest", 1, PACK)
 
-        def product(lhs_codes, lhs_scale, t, rhs_codes, rhs_scale, a, b, bank, dest, scale):
-            rows = slice(P * t, P * (t + 1))
+        def product(lhs_codes, lhs_scale, rhs_codes, rhs_scale, a, b, bank, dest, scale):
             acc = psum.tile([P, b - a], F32, name="acc", tag="bank%d" % bank)
-            nc.tensor.matmul_mx(out=acc[:], lhsT=lhs_codes[:, rows].bitcast(FP8X4), lhsT_scale=lhs_scale[:, rows], rhs=rhs_codes[:, a:b].bitcast(FP8X4), rhs_scale=rhs_scale[:, a:b], start=True, stop=True)
+            nc.tensor.matmul_mx(out=acc[:], lhsT=lhs_codes.bitcast(FP8X4), lhsT_scale=lhs_scale, rhs=rhs_codes[:, a:b].bitcast(FP8X4), rhs_scale=rhs_scale[:, a:b], start=True, stop=True)
             nc.scalar.activation(dest[:, a:b], acc[:], COPY, scale=scale)
 
         h = [keep.tile([P, 2 * S], F32, name="h%d" % t) for t in range(PACK)]
         for t in range(PACK):
-            product(d_codes, d_scale, t, xq_words, xq_scale, 0, S, t, h[t], gs_size[:, t : t + 1])
+            product(d_codes[t], d_scale[:, P * t : P * (t + 1)], xq_words, xq_scale, 0, S, t, h[t], gs_size[:, t : t + 1])
 
         c_scale_got = gather_packed(x_scale_win, cand_sb, U8, "c_scale_got", "after_d")
-        c_scale = deal(c_scale_got, U8, "c_scale")
+        c_scale = deal(c_scale_got, U8, "c_scale_first", 0, 1)
 
         st = [window("st", t) for t in range(PACK)]
-        z_grouped = [keep.tile([P, b - a, PACK], BF16, name="z_grouped%d" % a, align_bytes=64) for a, b in PIECES]
+        z_grouped = [keep.tile([P, b - a, PACK], BF16, name="z_grouped%d" % a, tag="z_grouped%d" % a, align_bytes=64) for a, b in PIECES]
         st_rounded = [keep.tile([P, S], BF16, name="st_rounded%d" % t) for t in range(PACK)]
         fetched = {}
 
@@ -126,12 +126,19 @@ def tile_picked_pqchopmnminmx_none_po_kernel(tc, x_words, x_scales, d_words, d_s
             regroup(z_grouped, least, t, a, b, gs_sign[:, t : t + 1])
 
         fetch(h, n1_sb, "n1", 0, 0, S)
+        fetch(h, n1_sb, "n1", 1, 0, S)
         larger(0)
-        for t in range(1, PACK):
-            fetch(h, n1_sb, "n1", t, 0, S)
-            fetch(st, n2_sb, "n2", t - 1, 0, S)
-            larger(t)
-            smaller_weighted(t - 1, 0, S)
+        larger(1)
+        fetch(st, n2_sb, "n2", 0, 0, S)
+        fetch(h, n1_sb, "n1", 2, 0, S)
+        smaller_weighted(0, 0, S)
+        fetch(st, n2_sb, "n2", 1, 0, S)
+        larger(2)
+        smaller_weighted(1, 0, S)
+        fetch(h, n1_sb, "n1", 3, 0, S)
+        fetch(st, n2_sb, "n2", 2, 0, S)
+        larger(3)
+        smaller_weighted(2, 0, S)
         first, second, third = PIECES
         fetch(st, n2_sb, "n2", LAST, *first)
         fetch(st, n2_sb, "n2", LAST, *second, tag="after_z")
@@ -151,10 +158,12 @@ def tile_picked_pqchopmnminmx_none_po_kernel(tc, x_words, x_scales, d_words, d_s
         for i, (a, b) in enumerate(PIECES):
             quantize(z_codes[:, a:b], z_scale[:, a:b], z_grouped[i])
             if i == 0:
-                c_codes = deal(c_words_got, U32, "c_codes")
-            product(c_codes, c_scale, 0, z_codes, z_scale, a, b, 4 + i, s[0], 0.0625)
+                c_codes = deal(c_words_got, U32, "c_codes_first", 0, 1)
+            product(c_codes[0], c_scale[0], z_codes, z_scale, a, b, 4 + i, s[0], 0.0625)
+        c_codes = c_codes + deal(c_words_got, U32, "c_codes_rest", 1, PACK, "z_grouped0")
+        c_scale = c_scale + deal(c_scale_got, U8, "c_scale_rest", 1, PACK, "z_grouped256")
         for t in range(1, PACK):
-            product(c_codes, c_scale, t, z_codes, z_scale, 0, S, (6 + t) % 8, s[t], 0.0625)
+            product(c_codes[t], c_scale[t], z_codes, z_scale, 0, S, (6 + t) % 8, s[t], 0.0625)
 
         out_rows = out_0.rearrange("(p t) c -> p t c", t=PACK)
         out_words = out_1[0].rearrange("p n t -> p (n t)").bitcast(I32)

@@ -12,13 +12,17 @@ U32 = mybir.dt.uint32
 U16 = mybir.dt.uint16
 U8 = mybir.dt.uint8
 FP8X4 = mybir.dt.float8_e4m3fn_x4
-COPY = mybir.ActivationFunctionType.Copy
+ACT = mybir.ActivationFunctionType
 MAX = mybir.AluOpType.max
 MIN = mybir.AluOpType.min
 
 P = 128
 PACK = 4
 LAST = PACK - 1
+LIST_ROWS = 16
+QUADRANT = 32
+BLOCK_ROWS = 8
+SIXTEENTH = 0.0625
 PIECES = ((0, 256), (256, 384), (384, 512))
 
 
@@ -29,176 +33,200 @@ def tile_picked_pqchopmnminmx_none_po_kernel(tc, x_words, x_scales, d_words, d_s
         psum = ctx.enter_context(tc.psum_pool(name="psum", bufs=1))
 
         def load_list(src, name):
-            tile = keep.tile([P, S // 16], U16, name=name)
-            nc.sync.dma_start(tile[:], src)
-            return tile
+            offsets = keep.tile([P, S // LIST_ROWS], U16, name=name)
+            nc.sync.dma_start(offsets[:], src)
+            return offsets
 
-        def picked(window, offsets, a, b):
-            return window[:].indirect(offsets[:, a // 16 : b // 16])
-
-        def window(name, t):
-            return keep.tile([P, S if t == LAST else 2 * S], F32, name="%s%d" % (name, t))
-
-        def deal(src, dtype, name, t0=0, t1=PACK, tag=None):
-            dealt = keep.tile([P, t1 - t0, P], dtype, name=name, tag=tag or name, align_bytes=64)
-            nc.vector.tensor_copy(dealt[:].rearrange("p t m -> p m t"), src[:].rearrange("p (m t) -> p m t", t=PACK)[:, :, t0:t1])
-            return [dealt[:, t, :] for t in range(t1 - t0)]
-
-        d_scale = keep.tile([P, H], U8, name="d_scale", align_bytes=64)
-        nc.gpsimd.memset(d_scale[:].bitcast(I32), 0)
-
-        k1_sb = load_list(k1, "k1_sb")
-        d_scale_win = keep.tile([P, G], U8, name="d_scale_win")
-        nc.sync.dma_start(d_scale_win[:].bitcast(I32), d_scales[0].bitcast(I32).unsqueeze(1).to_broadcast([16, 8, G // 4]))
-        offs_sb = load_list(offs, "offs_sb")
-        x_word_win = keep.tile([P, T], I32, name="x_word_win")
-        nc.sync.dma_start(x_word_win[:], x_words[0].rearrange("p n t -> p (n t)").bitcast(I32))
-        x_scale_win = keep.tile([P, T], U8, name="x_scale_win")
-        x_rows = x_scales[0].bitcast(I32)
-        for q in range(4):
-            nc.sync.dma_start(x_scale_win[:].bitcast(I32)[32 * q : 32 * q + 32, :], x_rows[4 * q : 4 * q + 4, :].unsqueeze(0).to_broadcast([8, 4, T // 4]))
-        d_word_win = keep.tile([P, G], I32, name="d_word_win")
-        nc.sync.dma_start(d_word_win[:], d_words[0].rearrange("p n t -> p (n t)").bitcast(I32))
-
-        gs_sb = keep.tile([P, PACK], F32, name="gs_sb")
-        nc.gpsimd.dma_start(gs_sb[:], gs.rearrange("(p t) o -> p (t o)", t=PACK))
-        gs_size = keep.tile([P, PACK], F32, name="gs_size")
-        gs_sign = keep.tile([P, PACK], F32, name="gs_sign")
-        nc.scalar.activation(gs_size[:], gs_sb[:], mybir.ActivationFunctionType.Abs, scale=0.0625)
-        nc.scalar.activation(gs_sign[:], gs_sb[:], mybir.ActivationFunctionType.Sign)
+        def window(name, spare):
+            return keep.tile([P, S + spare], F32, name=name)
 
         def gather_packed(table, offsets, dtype, name, tag):
             got = keep.tile([P, S], dtype, name=name, tag=tag, align_bytes=64)
             nc.vector.tensor_copy(got[:], table[:].bitcast(dtype).indirect(offsets[:]))
             return got
 
-        d_scale_got = gather_packed(d_scale_win, k1_sb, U8, "d_scale_got", "d_scale_got")
-        d_scale_dealt = keep.tile([P, H], U8, name="d_scale_dealt")
-        nc.vector.tensor_copy(d_scale_dealt[:].rearrange("p (t m) -> p m t", t=PACK), d_scale_got[:].rearrange("p (m t) -> p m t", t=PACK))
+        def deal(got, dtype, name, t0, t1, tag=None):
+            dealt = keep.tile([P, t1 - t0, P], dtype, name=name, tag=tag or name, align_bytes=64)
+            nc.vector.tensor_copy(dealt[:].rearrange("p t m -> p m t"), got[:].rearrange("p (m t) -> p m t", t=PACK)[:, :, t0:t1])
+            return dealt
+
+        def product(lhs_codes, lhs_scale, rhs_codes, rhs_scale, bank, dest, factor):
+            acc = psum.tile([P, dest.shape[1]], F32, name="acc", tag="bank%d" % bank)
+            nc.tensor.matmul_mx(out=acc[:], lhsT=lhs_codes.bitcast(FP8X4), lhsT_scale=lhs_scale, rhs=rhs_codes.bitcast(FP8X4), rhs_scale=rhs_scale, start=True, stop=True)
+            nc.scalar.activation(dest, acc[:], ACT.Copy, scale=factor)
+
+        def fetch(src, offsets, dtype, name, a, b, tag=None):
+            got = keep.tile([P, b - a], dtype, name=name, tag=tag or name, align_bytes=64)
+            nc.vector.tensor_copy(got[:], src[:].indirect(offsets[:, a // LIST_ROWS : b // LIST_ROWS]))
+            return got
+
+        def grouped_tiles(name):
+            return [keep.tile([P, b - a, PACK], BF16, name="%s%d" % (name, i), tag="%s%d" % (name, i), align_bytes=64) for i, (a, b) in enumerate(PIECES)]
+
+        def regroup(grouped, values, t, a, b, factor):
+            for i, (pa, pb) in enumerate(PIECES):
+                if a <= pa and pb <= b:
+                    nc.scalar.activation(grouped[i][:, :, t], values[:, pa - a : pb - a], ACT.Copy, scale=factor)
+
+        def quantize(codes, scales, grouped):
+            nc.vector.quantize_mx(out=codes.bitcast(FP8X4), scales=scales, in_=grouped[:].rearrange("p c t -> p (c t)"))
+
+        d_scale = keep.tile([P, H], U8, name="d_scale", align_bytes=64)
+        nc.gpsimd.memset(d_scale[:].bitcast(I32), 0)
+
+        k1_sb = load_list(k1, "k1_sb")
+        d_scale_table = keep.tile([P, G], U8, name="d_scale_table")
+        nc.sync.dma_start(d_scale_table[:].bitcast(I32), d_scales[0].bitcast(I32).unsqueeze(1).to_broadcast([P // BLOCK_ROWS, BLOCK_ROWS, G // 4]))
+        offs_sb = load_list(offs, "offs_sb")
+        x_word_table = keep.tile([P, T], I32, name="x_word_table")
+        nc.sync.dma_start(x_word_table[:], x_words[0].rearrange("p n t -> p (n t)").bitcast(I32))
+        x_scale_table = keep.tile([P, T], U8, name="x_scale_table")
+        x_scale_rows = x_scales[0].bitcast(I32)
+        for q in range(4):
+            nc.sync.dma_start(x_scale_table[:].bitcast(I32)[QUADRANT * q : QUADRANT * (q + 1), :], x_scale_rows[4 * q : 4 * q + 4, :].unsqueeze(0).to_broadcast([QUADRANT // 4, 4, T // 4]))
+        d_word_table = keep.tile([P, G], I32, name="d_word_table")
+        nc.sync.dma_start(d_word_table[:], d_words[0].rearrange("p n t -> p (n t)").bitcast(I32))
+
+        gs_sb = keep.tile([P, PACK], F32, name="gs_sb")
+        nc.gpsimd.dma_start(gs_sb[:], gs.rearrange("(p t) o -> p (t o)", t=PACK))
+        gs_size = keep.tile([P, PACK], F32, name="gs_size")
+        gs_sign = keep.tile([P, PACK], F32, name="gs_sign")
+        nc.scalar.activation(gs_size[:], gs_sb[:], ACT.Abs, scale=SIXTEENTH)
+        nc.scalar.activation(gs_sign[:], gs_sb[:], ACT.Sign)
+
+        d_scale_got = gather_packed(d_scale_table, k1_sb, U8, "d_scale_got", "d_scale_got")
+        d_scale_dealt = deal(d_scale_got, U8, "d_scale_dealt", 0, PACK)[:].rearrange("p t m -> p (t m)")
         for j in range(4):
-            nc.scalar.dma_start(d_scale[:].bitcast(I32)[j:P:32, :], d_scale_dealt[:].bitcast(I32)[8 * j : P : 32, :])
+            nc.scalar.dma_start(d_scale[:].bitcast(I32)[j:P:QUADRANT, :], d_scale_dealt.bitcast(I32)[BLOCK_ROWS * j : P : QUADRANT, :])
         cand_sb = load_list(cand, "cand_sb")
         n1_sb = load_list(n1, "n1_sb")
         n2_sb = load_list(n2, "n2_sb")
         n3_sb = load_list(n3, "n3_sb")
         n4_sb = load_list(n4, "n4_sb")
 
-        xq_words = gather_packed(x_word_win, offs_sb, U32, "xq_words", "xq_words")
-        xq_scale = gather_packed(x_scale_win, offs_sb, U8, "xq_scale", "xq_scale")
-        d_words_got = gather_packed(d_word_win, k1_sb, U32, "d_words_got", "after_d")
-        d_codes = deal(d_words_got, U32, "d_codes_first", 0, 1) + deal(d_words_got, U32, "d_codes_rest", 1, PACK)
+        xq_codes = gather_packed(x_word_table, offs_sb, U32, "xq_codes", "xq_codes")
+        xq_scale = gather_packed(x_scale_table, offs_sb, U8, "xq_scale", "xq_scale")
+        d_words_got = gather_packed(d_word_table, k1_sb, U32, "d_words_got", "behind_d_words")
+        d_codes_first = deal(d_words_got, U32, "d_codes_first", 0, 1)
+        d_codes_rest = deal(d_words_got, U32, "d_codes_rest", 1, PACK)
 
-        def product(lhs_codes, lhs_scale, rhs_codes, rhs_scale, a, b, bank, dest, scale):
-            acc = psum.tile([P, b - a], F32, name="acc", tag="bank%d" % bank)
-            nc.tensor.matmul_mx(out=acc[:], lhsT=lhs_codes.bitcast(FP8X4), lhsT_scale=lhs_scale, rhs=rhs_codes[:, a:b].bitcast(FP8X4), rhs_scale=rhs_scale[:, a:b], start=True, stop=True)
-            nc.scalar.activation(dest[:, a:b], acc[:], COPY, scale=scale)
-
-        h = [keep.tile([P, 2 * S], F32, name="h%d" % t) for t in range(PACK)]
+        h = [window("h%d" % t, S) for t in range(PACK)]
         for t in range(PACK):
-            product(d_codes[t], d_scale[:, P * t : P * (t + 1)], xq_words, xq_scale, 0, S, t, h[t], gs_size[:, t : t + 1])
+            lhs = d_codes_first[:, 0, :] if t == 0 else d_codes_rest[:, t - 1, :]
+            product(lhs, d_scale[:, P * t : P * (t + 1)], xq_codes[:], xq_scale[:], t, h[t][:, 0:S], gs_size[:, t : t + 1])
 
-        c_scale_got = gather_packed(x_scale_win, cand_sb, U8, "c_scale_got", "after_d")
-        c_scale = deal(c_scale_got, U8, "c_scale_first", 0, 1)
+        c_scale_got = gather_packed(x_scale_table, cand_sb, U8, "c_scale_got", "behind_d_words")
+        c_scale_first = deal(c_scale_got, U8, "c_scale_first", 0, 1)
 
-        st = [window("st", t) for t in range(PACK)]
-        z_grouped = [keep.tile([P, b - a, PACK], BF16, name="z_grouped%d" % a, tag="z_grouped%d" % a, align_bytes=64) for a, b in PIECES]
+        st = [window("st%d" % t, 0 if t == LAST else S) for t in range(PACK)]
         st_rounded = [keep.tile([P, S], BF16, name="st_rounded%d" % t) for t in range(PACK)]
-        fetched = {}
+        z_grouped = grouped_tiles("z_grouped")
+        h_at_n1, st_at_n2 = {}, {}
 
-        def fetch(src, offsets, name, t, a, b, tag=None):
-            dtype = BF16 if name == "n2" else F32
-            key = "%s_%d_%d" % (name, t, a)
-            fetched[name, t, a] = keep.tile([P, b - a], dtype, name=key, tag=tag or key, align_bytes=64)
-            nc.vector.tensor_copy(fetched[name, t, a][:], picked(src[t], offsets, a, b))
+        def fetch_n1(t):
+            h_at_n1[t] = fetch(h[t], n1_sb, F32, "h_at_n1_%d" % t, 0, S)
 
-        def regroup(grouped, values, t, a, b, scale):
-            for i, (pa, pb) in enumerate(PIECES):
-                if a <= pa and pb <= b:
-                    nc.scalar.activation(grouped[i][:, :, t], values[:, pa - a : pb - a], COPY, scale=scale)
-
-        def larger(t):
-            nc.vector.tensor_tensor(st[t][:, 0:S], h[t][:, 0:S], fetched["n1", t, 0][:], MAX)
+        def make_st(t):
+            nc.vector.tensor_tensor(st[t][:, 0:S], h[t][:, 0:S], h_at_n1[t][:], MAX)
             nc.scalar.copy(st_rounded[t][:], st[t][:, 0:S])
 
-        def smaller_weighted(t, a, b):
+        def fetch_n2(t, a, b, tag=None):
+            st_at_n2[t, a] = fetch(st[t], n2_sb, BF16, "st_at_n2_%d_%d" % (t, a), a, b, tag)
+
+        def make_z(t, a, b):
             least = keep.tile([P, b - a], BF16, name="least_%d_%d" % (t, a))
-            nc.vector.tensor_tensor(least[:], st_rounded[t][:, a:b], fetched["n2", t, a][:], MIN)
+            nc.vector.tensor_tensor(least[:], st_rounded[t][:, a:b], st_at_n2[t, a][:], MIN)
             regroup(z_grouped, least, t, a, b, gs_sign[:, t : t + 1])
 
-        fetch(h, n1_sb, "n1", 0, 0, S)
-        fetch(h, n1_sb, "n1", 1, 0, S)
-        larger(0)
-        larger(1)
-        fetch(st, n2_sb, "n2", 0, 0, S)
-        fetch(h, n1_sb, "n1", 2, 0, S)
-        smaller_weighted(0, 0, S)
-        fetch(st, n2_sb, "n2", 1, 0, S)
-        larger(2)
-        smaller_weighted(1, 0, S)
-        fetch(h, n1_sb, "n1", 3, 0, S)
-        fetch(st, n2_sb, "n2", 2, 0, S)
-        larger(3)
-        smaller_weighted(2, 0, S)
+        fetch_n1(0)
+        fetch_n1(1)
+        make_st(0)
+        make_st(1)
+        fetch_n2(0, 0, S)
+        fetch_n1(2)
+        make_z(0, 0, S)
+        fetch_n2(1, 0, S)
+        make_st(2)
+        make_z(1, 0, S)
+        fetch_n1(LAST)
+        fetch_n2(2, 0, S)
+        make_st(LAST)
+        make_z(2, 0, S)
         first, second, third = PIECES
-        fetch(st, n2_sb, "n2", LAST, *first)
-        fetch(st, n2_sb, "n2", LAST, *second, tag="after_z")
-        smaller_weighted(LAST, *first)
-        fetch(st, n2_sb, "n2", LAST, *third)
-        smaller_weighted(LAST, *second)
-        smaller_weighted(LAST, *third)
+        fetch_n2(LAST, *first)
+        fetch_n2(LAST, *second, tag="behind_z")
+        make_z(LAST, *first)
+        fetch_n2(LAST, *third)
+        make_z(LAST, *second)
+        make_z(LAST, *third)
 
         z_codes = keep.tile([P, S], U32, name="z_codes", align_bytes=64)
         z_scale = keep.tile([P, S], U8, name="z_scale", align_bytes=64)
+        c_words_got = gather_packed(x_word_table, cand_sb, U32, "c_words_got", "behind_z")
 
-        def quantize(codes, scales, grouped):
-            nc.vector.quantize_mx(out=codes.bitcast(FP8X4), scales=scales, in_=grouped[:].rearrange("p c t -> p (c t)"))
-
-        c_words_got = gather_packed(x_word_win, cand_sb, U32, "c_words_got", "after_z")
-        s = [window("s", t) for t in range(PACK)]
+        s = [window("s%d" % t, 0 if t == LAST else S) for t in range(PACK)]
         for i, (a, b) in enumerate(PIECES):
             quantize(z_codes[:, a:b], z_scale[:, a:b], z_grouped[i])
             if i == 0:
-                c_codes = deal(c_words_got, U32, "c_codes_first", 0, 1)
-            product(c_codes[0], c_scale[0], z_codes, z_scale, a, b, 4 + i, s[0], 0.0625)
-        c_codes = c_codes + deal(c_words_got, U32, "c_codes_rest", 1, PACK, "z_grouped0")
-        c_scale = c_scale + deal(c_scale_got, U8, "c_scale_rest", 1, PACK, "z_grouped256")
+                c_codes_first = deal(c_words_got, U32, "c_codes_first", 0, 1)
+            product(c_codes_first[:, 0, :], c_scale_first[:, 0, :], z_codes[:, a:b], z_scale[:, a:b], PACK + i, s[0][:, a:b], SIXTEENTH)
+        c_codes_rest = deal(c_words_got, U32, "c_codes_rest", 1, PACK, "z_grouped0")
+        c_scale_rest = deal(c_scale_got, U8, "c_scale_rest", 1, PACK, "z_grouped1")
         for t in range(1, PACK):
-            product(c_codes[t], c_scale[t], z_codes, z_scale, 0, S, (6 + t) % 8, s[t], 0.0625)
+            product(c_codes_rest[:, t - 1, :], c_scale_rest[:, t - 1, :], z_codes[:], z_scale[:], (6 + t) % 8, s[t][:, 0:S], SIXTEENTH)
 
         out_rows = out_0.rearrange("(p t) c -> p t c", t=PACK)
         out_words = out_1[0].rearrange("p n t -> p (n t)").bitcast(I32)
         out_scale = keep.tile([P, S], U8, name="out_scale", align_bytes=64)
-        out_grouped = [keep.tile([P, b - a, PACK], BF16, name="out_grouped%d" % a, align_bytes=64) for a, b in PIECES]
-        upper = {}
+        out_grouped = grouped_tiles("out_grouped")
+        s_at_n3, s_at_n4, larger = {}, {}, {}
 
-        def raise_to_n3(t, a, b):
-            upper[t, a] = keep.tile([P, b - a], F32, name="upper_%d_%d" % (t, a))
-            nc.vector.tensor_tensor(upper[t, a][:], s[t][:, a:b], fetched["n3", t, a][:], MAX)
+        def fetch_n3(t, a, b):
+            s_at_n3[t, a] = fetch(s[t], n3_sb, F32, "s_at_n3_%d_%d" % (t, a), a, b)
 
-        def cap_at_n4(t, a, b):
+        def fetch_n4(t, a, b):
+            s_at_n4[t, a] = fetch(s[t], n4_sb, F32, "s_at_n4_%d_%d" % (t, a), a, b)
+
+        def make_larger(t, a, b):
+            larger[t, a] = keep.tile([P, b - a], F32, name="larger_%d_%d" % (t, a))
+            nc.vector.tensor_tensor(larger[t, a][:], s[t][:, a:b], s_at_n3[t, a][:], MAX)
+
+        def make_out(t, a, b):
             result = keep.tile([P, b - a], F32, name="result_%d_%d" % (t, a))
-            nc.vector.tensor_tensor(result[:], upper[t, a][:], fetched["n4", t, a][:], MIN)
+            nc.vector.tensor_tensor(result[:], larger[t, a][:], s_at_n4[t, a][:], MIN)
             regroup(out_grouped, result, t, a, b, 1.0)
             nc.sync.dma_start(out_rows[:, t, a:b], result[:])
 
-        def hand_out(i):
+        def quantize_out(i):
             a, b = PIECES[i]
             codes = keep.tile([P, b - a], I32, name="out_codes%d" % i, align_bytes=64)
             quantize(codes[:], out_scale[:, a:b], out_grouped[i])
             nc.sync.dma_start(out_words[:, a:b], codes[:])
 
-        steps = [(t, 0, S) for t in range(LAST)] + [(LAST, a, b) for a, b in PIECES]
-        for n, step in enumerate(steps):
-            fetch(s, n3_sb, "n3", *step)
-            if n > 0:
-                cap_at_n4(*steps[n - 1])
-            fetch(s, n4_sb, "n4", *step)
-            raise_to_n3(*step)
-        hand_out(0)
-        cap_at_n4(*steps[-1])
-        hand_out(1)
-        hand_out(2)
-        scale_rows = out_2[0].bitcast(I32)
+        for t in range(LAST):
+            fetch_n3(t, 0, S)
+            if t > 0:
+                make_out(t - 1, 0, S)
+            fetch_n4(t, 0, S)
+            make_larger(t, 0, S)
+        fetch_n3(LAST, *first)
+        make_out(LAST - 1, 0, S)
+        fetch_n4(LAST, *first)
+        fetch_n3(LAST, *second)
+        make_larger(LAST, *first)
+        fetch_n3(LAST, *third)
+        make_out(LAST, *first)
+        make_larger(LAST, *second)
+        fetch_n4(LAST, *second)
+        make_larger(LAST, *third)
+        make_out(LAST, *second)
+        fetch_n4(LAST, *third)
+        quantize_out(0)
+        make_out(LAST, *third)
+        quantize_out(1)
+        quantize_out(2)
+
+        out_scale_rows = out_2[0].bitcast(I32)
         for q in range(4):
             queue = nc.scalar if q % 2 == 0 else nc.sync
-            queue.dma_start(scale_rows[4 * q : 4 * q + 4, :], out_scale[:].bitcast(I32)[32 * q : 32 * q + 4, :])
+            queue.dma_start(out_scale_rows[4 * q : 4 * q + 4, :], out_scale[:].bitcast(I32)[QUADRANT * q : QUADRANT * q + 4, :])

from contextlib import ExitStack

import concourse.mybir as mybir

K, T, S, G, H, C = 512, 1024, 512, 2048, 512, 512
FLOPS = 2 * K * H * S + 2 * K * C * S

F32 = mybir.dt.float32
BF16 = mybir.dt.bfloat16
I32 = mybir.dt.int32
U32 = mybir.dt.uint32
U16 = mybir.dt.uint16
U8 = mybir.dt.uint8
FP8X4 = mybir.dt.float8_e4m3fn_x4
ACT = mybir.ActivationFunctionType
MAX = mybir.AluOpType.max
MIN = mybir.AluOpType.min

P = 128
PACK = 4
LAST = PACK - 1
LIST_ROWS = 16
QUADRANT = 32
BLOCK_ROWS = 8
SIXTEENTH = 0.0625
PIECES = ((0, 256), (256, 384), (384, 512))


def tile_picked_pqchopmnminmx_none_po_kernel(tc, x_words, x_scales, d_words, d_scales, gs, offs, k1, n1, n2, cand, n3, n4, out_0, out_1, out_2):
    nc = tc.nc
    with ExitStack() as ctx:
        keep = ctx.enter_context(tc.tile_pool(name="keep", bufs=1))
        psum = ctx.enter_context(tc.psum_pool(name="psum", bufs=1))

        def load_list(src, name):
            offsets = keep.tile([P, S // LIST_ROWS], U16, name=name)
            nc.sync.dma_start(offsets[:], src)
            return offsets

        def window(name, spare):
            return keep.tile([P, S + spare], F32, name=name)

        def gather_packed(table, offsets, dtype, name, tag):
            got = keep.tile([P, S], dtype, name=name, tag=tag, align_bytes=64)
            nc.vector.tensor_copy(got[:], table[:].bitcast(dtype).indirect(offsets[:]))
            return got

        def deal(got, dtype, name, t0, t1, tag=None):
            dealt = keep.tile([P, t1 - t0, P], dtype, name=name, tag=tag or name, align_bytes=64)
            nc.vector.tensor_copy(dealt[:].rearrange("p t m -> p m t"), got[:].rearrange("p (m t) -> p m t", t=PACK)[:, :, t0:t1])
            return dealt

        def product(lhs_codes, lhs_scale, rhs_codes, rhs_scale, bank, dest, factor):
            acc = psum.tile([P, dest.shape[1]], F32, name="acc", tag="bank%d" % bank)
            nc.tensor.matmul_mx(out=acc[:], lhsT=lhs_codes.bitcast(FP8X4), lhsT_scale=lhs_scale, rhs=rhs_codes.bitcast(FP8X4), rhs_scale=rhs_scale, start=True, stop=True)
            nc.scalar.activation(dest, acc[:], ACT.Copy, scale=factor)

        def fetch(src, offsets, dtype, name, a, b, tag=None):
            got = keep.tile([P, b - a], dtype, name=name, tag=tag or name, align_bytes=64)
            nc.vector.tensor_copy(got[:], src[:].indirect(offsets[:, a // LIST_ROWS : b // LIST_ROWS]))
            return got

        def grouped_tiles(name):
            return [keep.tile([P, b - a, PACK], BF16, name="%s%d" % (name, i), tag="%s%d" % (name, i), align_bytes=64) for i, (a, b) in enumerate(PIECES)]

        def regroup(grouped, values, t, a, b, factor):
            for i, (pa, pb) in enumerate(PIECES):
                if a <= pa and pb <= b:
                    nc.scalar.activation(grouped[i][:, :, t], values[:, pa - a : pb - a], ACT.Copy, scale=factor)

        def quantize(codes, scales, grouped):
            nc.vector.quantize_mx(out=codes.bitcast(FP8X4), scales=scales, in_=grouped[:].rearrange("p c t -> p (c t)"))

        d_scale = keep.tile([P, H], U8, name="d_scale", align_bytes=64)
        nc.gpsimd.memset(d_scale[:].bitcast(I32), 0)

        k1_sb = load_list(k1, "k1_sb")
        d_scale_table = keep.tile([P, G], U8, name="d_scale_table")
        nc.sync.dma_start(d_scale_table[:].bitcast(I32), d_scales[0].bitcast(I32).unsqueeze(1).to_broadcast([P // BLOCK_ROWS, BLOCK_ROWS, G // 4]))
        offs_sb = load_list(offs, "offs_sb")
        x_word_table = keep.tile([P, T], I32, name="x_word_table")
        nc.sync.dma_start(x_word_table[:], x_words[0].rearrange("p n t -> p (n t)").bitcast(I32))
        x_scale_table = keep.tile([P, T], U8, name="x_scale_table")
        x_scale_rows = x_scales[0].bitcast(I32)
        for q in range(4):
            nc.sync.dma_start(x_scale_table[:].bitcast(I32)[QUADRANT * q : QUADRANT * (q + 1), :], x_scale_rows[4 * q : 4 * q + 4, :].unsqueeze(0).to_broadcast([QUADRANT // 4, 4, T // 4]))
        d_word_table = keep.tile([P, G], I32, name="d_word_table")
        nc.sync.dma_start(d_word_table[:], d_words[0].rearrange("p n t -> p (n t)").bitcast(I32))

        gs_sb = keep.tile([P, PACK], F32, name="gs_sb")
        nc.gpsimd.dma_start(gs_sb[:], gs.rearrange("(p t) o -> p (t o)", t=PACK))
        gs_size = keep.tile([P, PACK], F32, name="gs_size")
        gs_sign = keep.tile([P, PACK], F32, name="gs_sign")
        nc.scalar.activation(gs_size[:], gs_sb[:], ACT.Abs, scale=SIXTEENTH)
        nc.scalar.activation(gs_sign[:], gs_sb[:], ACT.Sign)

        d_scale_got = gather_packed(d_scale_table, k1_sb, U8, "d_scale_got", "d_scale_got")
        d_scale_dealt = deal(d_scale_got, U8, "d_scale_dealt", 0, PACK)[:].rearrange("p t m -> p (t m)")
        for j in range(4):
            nc.scalar.dma_start(d_scale[:].bitcast(I32)[j:P:QUADRANT, :], d_scale_dealt.bitcast(I32)[BLOCK_ROWS * j : P : QUADRANT, :])
        cand_sb = load_list(cand, "cand_sb")
        n1_sb = load_list(n1, "n1_sb")
        n2_sb = load_list(n2, "n2_sb")
        n3_sb = load_list(n3, "n3_sb")
        n4_sb = load_list(n4, "n4_sb")

        xq_codes = gather_packed(x_word_table, offs_sb, U32, "xq_codes", "xq_codes")
        xq_scale = gather_packed(x_scale_table, offs_sb, U8, "xq_scale", "xq_scale")
        d_words_got = gather_packed(d_word_table, k1_sb, U32, "d_words_got", "behind_d_words")
        d_codes_first = deal(d_words_got, U32, "d_codes_first", 0, 1)
        d_codes_rest = deal(d_words_got, U32, "d_codes_rest", 1, PACK)

        h = [window("h%d" % t, S) for t in range(PACK)]
        for t in range(PACK):
            lhs = d_codes_first[:, 0, :] if t == 0 else d_codes_rest[:, t - 1, :]
            product(lhs, d_scale[:, P * t : P * (t + 1)], xq_codes[:], xq_scale[:], t, h[t][:, 0:S], gs_size[:, t : t + 1])

        c_scale_got = gather_packed(x_scale_table, cand_sb, U8, "c_scale_got", "behind_d_words")
        c_scale_first = deal(c_scale_got, U8, "c_scale_first", 0, 1)

        st = [window("st%d" % t, 0 if t == LAST else S) for t in range(PACK)]
        st_rounded = [keep.tile([P, S], BF16, name="st_rounded%d" % t) for t in range(PACK)]
        z_grouped = grouped_tiles("z_grouped")
        h_at_n1, st_at_n2 = {}, {}

        def fetch_n1(t):
            h_at_n1[t] = fetch(h[t], n1_sb, F32, "h_at_n1_%d" % t, 0, S)

        def make_st(t):
            nc.vector.tensor_tensor(st[t][:, 0:S], h[t][:, 0:S], h_at_n1[t][:], MAX)
            nc.scalar.copy(st_rounded[t][:], st[t][:, 0:S])

        def fetch_n2(t, a, b, tag=None):
            st_at_n2[t, a] = fetch(st[t], n2_sb, BF16, "st_at_n2_%d_%d" % (t, a), a, b, tag)

        def make_z(t, a, b):
            least = keep.tile([P, b - a], BF16, name="least_%d_%d" % (t, a))
            nc.vector.tensor_tensor(least[:], st_rounded[t][:, a:b], st_at_n2[t, a][:], MIN)
            regroup(z_grouped, least, t, a, b, gs_sign[:, t : t + 1])

        fetch_n1(0)
        fetch_n1(1)
        make_st(0)
        make_st(1)
        fetch_n2(0, 0, S)
        fetch_n1(2)
        make_z(0, 0, S)
        fetch_n2(1, 0, S)
        make_st(2)
        make_z(1, 0, S)
        fetch_n1(LAST)
        fetch_n2(2, 0, S)
        make_st(LAST)
        make_z(2, 0, S)
        first, second, third = PIECES
        fetch_n2(LAST, *first)
        fetch_n2(LAST, *second, tag="behind_z")
        make_z(LAST, *first)
        fetch_n2(LAST, *third)
        make_z(LAST, *second)
        make_z(LAST, *third)

        z_codes = keep.tile([P, S], U32, name="z_codes", align_bytes=64)
        z_scale = keep.tile([P, S], U8, name="z_scale", align_bytes=64)
        c_words_got = gather_packed(x_word_table, cand_sb, U32, "c_words_got", "behind_z")

        s = [window("s%d" % t, 0 if t == LAST else S) for t in range(PACK)]
        for i, (a, b) in enumerate(PIECES):
            quantize(z_codes[:, a:b], z_scale[:, a:b], z_grouped[i])
            if i == 0:
                c_codes_first = deal(c_words_got, U32, "c_codes_first", 0, 1)
            product(c_codes_first[:, 0, :], c_scale_first[:, 0, :], z_codes[:, a:b], z_scale[:, a:b], PACK + i, s[0][:, a:b], SIXTEENTH)
        c_codes_rest = deal(c_words_got, U32, "c_codes_rest", 1, PACK, "z_grouped0")
        c_scale_rest = deal(c_scale_got, U8, "c_scale_rest", 1, PACK, "z_grouped1")
        for t in range(1, PACK):
            product(c_codes_rest[:, t - 1, :], c_scale_rest[:, t - 1, :], z_codes[:], z_scale[:], (6 + t) % 8, s[t][:, 0:S], SIXTEENTH)

        out_rows = out_0.rearrange("(p t) c -> p t c", t=PACK)
        out_words = out_1[0].rearrange("p n t -> p (n t)").bitcast(I32)
        out_scale = keep.tile([P, S], U8, name="out_scale", align_bytes=64)
        out_grouped = grouped_tiles("out_grouped")
        s_at_n3, s_at_n4, larger = {}, {}, {}

        def fetch_n3(t, a, b):
            s_at_n3[t, a] = fetch(s[t], n3_sb, F32, "s_at_n3_%d_%d" % (t, a), a, b)

        def fetch_n4(t, a, b):
            s_at_n4[t, a] = fetch(s[t], n4_sb, F32, "s_at_n4_%d_%d" % (t, a), a, b)

        def make_larger(t, a, b):
            larger[t, a] = keep.tile([P, b - a], F32, name="larger_%d_%d" % (t, a))
            nc.vector.tensor_tensor(larger[t, a][:], s[t][:, a:b], s_at_n3[t, a][:], MAX)

        def make_out(t, a, b):
            result = keep.tile([P, b - a], F32, name="result_%d_%d" % (t, a))
            nc.vector.tensor_tensor(result[:], larger[t, a][:], s_at_n4[t, a][:], MIN)
            regroup(out_grouped, result, t, a, b, 1.0)
            nc.sync.dma_start(out_rows[:, t, a:b], result[:])

        def quantize_out(i):
            a, b = PIECES[i]
            codes = keep.tile([P, b - a], I32, name="out_codes%d" % i, align_bytes=64)
            quantize(codes[:], out_scale[:, a:b], out_grouped[i])
            nc.sync.dma_start(out_words[:, a:b], codes[:])

        for t in range(LAST):
            fetch_n3(t, 0, S)
            if t > 0:
                make_out(t - 1, 0, S)
            fetch_n4(t, 0, S)
            make_larger(t, 0, S)
        fetch_n3(LAST, *first)
        make_out(LAST - 1, 0, S)
        fetch_n4(LAST, *first)
        fetch_n3(LAST, *second)
        make_larger(LAST, *first)
        fetch_n3(LAST, *third)
        make_out(LAST, *first)
        make_larger(LAST, *second)
        fetch_n4(LAST, *second)
        make_larger(LAST, *third)
        make_out(LAST, *second)
        fetch_n4(LAST, *third)
        quantize_out(0)
        make_out(LAST, *third)
        quantize_out(1)
        quantize_out(2)

        out_scale_rows = out_2[0].bitcast(I32)
        for q in range(4):
            queue = nc.scalar if q % 2 == 0 else nc.sync
            queue.dma_start(out_scale_rows[4 * q : 4 * q + 4, :], out_scale[:].bitcast(I32)[QUADRANT * q : QUADRANT * q + 4, :])
